import numpy as np
import ml_dtypes


def mxq(x, axis, fmt="e4m3"):
    dtype, down = {"e4m3": (ml_dtypes.float8_e4m3fn, 7), "e5m2": (ml_dtypes.float8_e5m2, 14)}[fmt]
    v = np.moveaxis(np.asarray(x, np.float32).astype(ml_dtypes.bfloat16).astype(np.float64), axis, -1)
    blocks = v.reshape(v.shape[:-1] + (-1, 32))
    amax = np.abs(blocks).max(-1, keepdims=True)
    byte = np.maximum(np.where(amax > 0, np.frexp(amax)[1] - 1 + 127, 0) - down, 1)
    scale = np.exp2(byte - 127.0)
    codes = (blocks / scale).astype(np.float32).astype(dtype).astype(np.float64)
    return np.moveaxis((codes * scale).reshape(v.shape), -1, axis)


WIDE = False


def mx_kscale(k):
    if not WIDE:
        return np.ones(k)
    levels = np.array([30, -30])
    if k % 512:
        return np.exp2(np.random.permutation(np.resize(levels, k // 32))).repeat(32)
    a = np.empty((k // 512, 16))
    for p in range(k // 512):
        a[p, :8] = np.random.permutation(np.resize(levels, 8))
        for g in range(8):
            far = levels[np.abs(levels - a[p, g]) >= 10]
            a[p, g + 8] = far[np.random.randint(len(far))]
    return np.exp2(a.ravel()).repeat(32)


def f64(x):
    return np.asarray(x).astype(np.float64)


def striped(idx):
    return np.tile(np.asarray(idx).reshape(-1, 16).T, (8, 1)).astype(np.uint16)


def unstriped(offs):
    return offs[:16].T.reshape(-1).astype(np.int64)


E2M1 = np.array([0.0, 0.5, 1.0, 1.5, 2.0, 3.0, 4.0, 6.0, -0.0, -0.5, -1.0, -1.5, -2.0, -3.0, -4.0, -6.0])


def pack_weight(w, fmt):
    k, n = w.shape
    w = f64(np.asarray(w, np.float32).astype(ml_dtypes.bfloat16)).reshape(k // 32, 32, n)
    amax = np.abs(w).max(1)
    if fmt in ("e4m3", "e5m2"):
        byte = np.frexp(amax)[1] - 1 + 127 - (7 if fmt == "e4m3" else 14)
    else:
        mant, ex = np.frexp(amax / 6.0)
        byte = np.where(mant > 0.5, ex, ex - 1) + 127
    byte = np.clip(np.where(amax > 0, byte, 1), 1, 254)
    scaled = (w * np.exp2(127.0 - byte)[:, None, :]).reshape(k, n).astype(np.float32)
    by_word = np.ascontiguousarray(scaled.reshape(k // 512, 128, 4, n).transpose(0, 1, 3, 2))
    if fmt in ("e4m3", "e5m2"):
        words = by_word.astype(ml_dtypes.float8_e4m3fn if fmt == "e4m3" else ml_dtypes.float8_e5m2).view(np.uint8)
    else:
        c = by_word.astype(ml_dtypes.float4_e2m1fn).view(np.uint8) & 0xF
        words = (c[..., 0::2] | (c[..., 1::2] << 4)).reshape(k // 512, 128, 2 * n)
    return np.ascontiguousarray(words), np.ascontiguousarray(byte.astype(np.uint8).reshape(k // 512, 16, n))


def unpack_weight(words, scales, fmt):
    g, _, n = scales.shape
    words = np.ascontiguousarray(words).reshape(g, 128, n, -1)
    if fmt in ("e4m3", "e5m2"):
        vals = words.view(ml_dtypes.float8_e4m3fn if fmt == "e4m3" else ml_dtypes.float8_e5m2).astype(np.float64)
    else:
        nib = np.empty((g, 128, n, 4), np.uint8)
        nib[..., 0::2] = words & 0xF
        nib[..., 1::2] = words >> 4
        vals = E2M1[nib]
    vals = vals * np.repeat(np.exp2(scales.astype(np.float64) - 127.0), 8, axis=1)[..., None]
    return vals.transpose(0, 1, 3, 2).reshape(g * 512, n)


def e4m3fn_bytes(y):
    return np.clip(np.asarray(y, np.float64), -448.0, 448.0).astype(np.float32).astype(ml_dtypes.float8_e4m3fn).view(np.uint8)


def e4m3fn_values(b):
    return np.asarray(b, np.uint8).view(ml_dtypes.float8_e4m3fn).astype(np.float64)


K, T, J, R, V, D, U, E = 512, 2048, 256, 512, 1024, 1024, 256, 512


def setup_inputs():
    n = np.random.standard_normal
    idx = np.random.permutation(T)[:J]
    idx2 = np.random.permutation(T)[:J]
    idx3 = np.random.permutation(V)[:U]
    idx4 = np.random.permutation(D)[:U]
    idx5 = np.random.permutation(E)[:U]
    fk = mx_kscale(K)
    fr = mx_kscale(R)
    xtp = pack_weight(n((K, T)) / fk[:, None], "e2m1")
    wp = pack_weight(n((K, R)) * 1 / np.sqrt(K) * fk[:, None] * fr, "e4m3")
    w2p = pack_weight(n((K, R)) * 1 / np.sqrt(K) * fk[:, None] * fr, "e5m2")
    return {
        "xt_words": xtp[0],
        "xt_scales": xtp[1],
        "w_words": wp[0],
        "w_scales": wp[1],
        "w2_words": w2p[0],
        "w2_scales": w2p[1],
        "ca": e4m3fn_bytes(60.0 * n((R, V))),
        "cb": e4m3fn_bytes(60.0 * n((R, D))),
        "sa": (np.random.uniform(0.0002, 0.0006, (R, 1)) / fr[:, None]).astype(np.float32),
        "sb": (np.random.uniform(0.0002, 0.0006, (R, 1)) / fr[:, None]).astype(np.float32),
        "sz": (np.random.uniform(0.5, 1.6, (J, 1))).astype(np.float32),
        "offs": striped(idx),
        "offs2": striped(idx2),
        "offs3": striped(idx3),
        "offs4": striped(idx4),
        "offs5": striped(idx5),
    }


def reference(xt_words, xt_scales, w_words, w_scales, w2_words, w2_scales, ca, cb, sa, sb, sz, offs, offs2, offs3, offs4, offs5):
    idx = unstriped(offs)
    idx2 = unstriped(offs2)
    idx3 = unstriped(offs3)
    idx4 = unstriped(offs4)
    idx5 = unstriped(offs5)
    xtu = unpack_weight(xt_words, xt_scales, "e2m1")
    wu = unpack_weight(w_words, w_scales, "e4m3")
    w2u = unpack_weight(w2_words, w2_scales, "e5m2")
    xtidxg = xtu[:, idx]
    a = wu.T @ xtidxg
    xtidx2g = xtu[:, idx2]
    b = w2u.T @ xtidx2g
    ka = e4m3fn_values(ca)[:, idx3] * f64(sa)
    kb = e4m3fn_values(cb)[:, idx4] * f64(sb)
    aq = mxq(a, 0, "e4m3")
    kaq = mxq(ka, 0, "e4m3")
    bq = mxq(b, 0, "e4m3")
    kbq = mxq(kb, 0, "e4m3")
    p = aq.T @ kaq + bq.T @ kbq
    y = np.zeros((J, E))
    y[:, idx5] = p * f64(sz)
    return y

@@ -1,0 +1,170 @@
+from contextlib import ExitStack
+
+import concourse.mybir as mybir
+
+K, T, J, R, V, U, E = 512, 2048, 256, 512, 1024, 256, 512
+FLOPS = 2 * (2 * K * R * J) + 2 * (2 * R * J * U)
+
+F32 = mybir.dt.float32
+BF16 = mybir.dt.bfloat16
+I32 = mybir.dt.int32
+U32 = mybir.dt.uint32
+U16 = mybir.dt.uint16
+U8 = mybir.dt.uint8
+F8 = mybir.dt.float8_e4m3fn
+E4M3X4 = mybir.dt.float8_e4m3fn_x4
+E5M2X4 = mybir.dt.float8_e5m2_x4
+E2M1X4 = mybir.dt.float4_e2m1fn_x4
+COPY = mybir.ActivationFunctionType.Copy
+MULT = mybir.AluOpType.mult
+
+P = 128
+H = 128
+
+
+def tile_list_scoredboth_kernel(tc, xt_words, xt_scales, w_words, w_scales, w2_words, w2_scales,
+                                   ca, cb, sa, sb, sz, offs, offs2, offs3, offs4, offs5, out):
+    nc = tc.nc
+    with ExitStack() as ctx:
+        pool = ctx.enter_context(tc.tile_pool(name="held", bufs=1))
+        psum = ctx.enter_context(tc.psum_pool(name="psum", bufs=1))
+
+        def sb_tile(name, shape, dtype, tag=None):
+            return pool.tile(shape, dtype, name=name, tag=tag or name, align_bytes=64)
+
+        def load_list(name, src):
+            tile = sb_tile(name, [P, 16], U16)
+            nc.sync.dma_start(tile[:], src)
+            return tile
+
+        def load_table(name, src, t):
+            tile = sb_tile(name, [P, V], U8)
+            nc.sync.dma_start(tile[:], src.rearrange("(p t) v -> p t v", t=4)[:, t, :])
+            return tile
+
+        def cleared_plane(engine, name, width):
+            tile = sb_tile(name, [P, width], U8)
+            engine.memset(tile[:].bitcast(I32), 0)
+            return tile
+
+        def load_plane(queue, plane, src):
+            for q in range(4):
+                queue.dma_start(plane[32 * q:32 * q + 4, :].bitcast(I32), src[0, 4 * q:4 * q + 4, :].bitcast(I32))
+
+        def load_words(name, src):
+            tile = sb_tile(name, [P, R], U32)
+            nc.sync.dma_start(tile[:].bitcast(I32), src[0].rearrange("p n t -> p (n t)").bitcast(I32))
+            return tile
+
+        xs = cleared_plane(nc.gpsimd, "xs", T)
+        ws_raw = cleared_plane(nc.vector, "ws_raw", R)
+        w2s_raw = cleared_plane(nc.vector, "w2s_raw", R)
+        pages = [sb_tile(f"page{h}", [P, E], F32) for h in range(2)]
+        for h in range(2):
+            nc.vector.memset(pages[h][:], 0.0)
+
+        sb_t = sb_tile("sb_t", [P, 4], F32)
+        nc.gpsimd.dma_start(sb_t[:], sb.rearrange("(p t) o -> p (t o)", t=4))
+        sz_t = sb_tile("sz_t", [P, 2], F32)
+        with nc.allow_non_contiguous_dma(reason="one weight a partition"):
+            nc.gpsimd.dma_start(sz_t[:], sz.rearrange("(h p) o -> p (h o)", h=2))
+
+        l3 = load_list("l3", offs3)
+        ca_t = [load_table("ca0", ca, 0)]
+        sa_t = sb_tile("sa_t", [P, 4], F32)
+        nc.sync.dma_start(sa_t[:], sa.rearrange("(p t) o -> p (t o)", t=4))
+        ca_t.extend(load_table(f"ca{t}", ca, t) for t in range(1, 4))
+        xw = sb_tile("xw", [P, T], U16)
+        nc.sync.dma_start(xw[:].bitcast(I32), xt_words[0].bitcast(I32))
+        l1 = load_list("l1", offs)
+        load_plane(nc.sync, xs, xt_scales)
+        w_raw = load_words("w_raw", w_words)
+        load_plane(nc.sync, ws_raw, w_scales)
+        l2 = load_list("l2", offs2)
+        w2_raw = load_words("w2_raw", w2_words)
+        load_plane(nc.sync, w2s_raw, w2_scales)
+        l4 = load_list("l4", offs4)
+        cb_t = [load_table(f"cb{t}", cb, t) for t in range(4)]
+        l5 = load_list("l5", offs5)
+
+        def quantize(name, src, n):
+            words = sb_tile(name + "_w", [P, n], U32)
+            scales = sb_tile(name + "_s", [P, n], U8)
+            nc.vector.quantize_mx(out=words[:].bitcast(E4M3X4), scales=scales[:], in_=src)
+            return words, scales
+
+        def interleave(engine_copy, dst, src):
+            engine_copy(dst[:].rearrange("p (c i t) -> p c t i", i=4, t=4),
+                        src[:].rearrange("p t (c i) -> p c t i", i=4))
+
+        ka_rows = sb_tile("ka_rows", [P, 4, U], BF16)
+        for t in range(4):
+            g = sb_tile(f"ga{t}", [P, U], U8)
+            nc.vector.tensor_copy(g[:], ca_t[t][:].indirect(l3[:]))
+            nc.scalar.activation(ka_rows[:, t, :], g[:].bitcast(F8), COPY, scale=sa_t[:, t:t + 1])
+        ka_il = sb_tile("ka_il", [P, 4 * U], BF16)
+        interleave(nc.scalar.copy, ka_il, ka_rows)
+
+        def first_stage(name, lst, raw_words, raw_plane, fmt):
+            gw = sb_tile(name + "_gw", [P, J], U16)
+            nc.vector.tensor_copy(gw[:], xw[:].indirect(lst[:]))
+            gs = sb_tile(name + "_gs", [P, J], U8)
+            nc.vector.tensor_copy(gs[:], xs[:].indirect(lst[:]))
+            words = sb_tile(name + "_words", [P, R], U32)
+            nc.scalar.copy(words[:].rearrange("p (t c i) -> p c t i", t=4, i=4),
+                           raw_words[:].rearrange("p (c i t) -> p c t i", t=4, i=4))
+            plane = sb_tile(name + "_plane", [P, R], U8)
+            nc.vector.tensor_copy(plane[:].rearrange("p (t m) -> p t m", t=4),
+                                  raw_plane[:].rearrange("p (m t) -> p t m", t=4))
+            rounded = sb_tile(name + "_bf", [P, 4 * J], BF16)
+            for h in range(2):
+                bank = psum.tile([P, 4, H], F32, name=f"{name}_bank{h}")
+                for t in range(4):
+                    nc.tensor.matmul_mx(out=bank[:, t, :],
+                                        lhsT=words[:, H * t:H * (t + 1)].bitcast(fmt),
+                                        lhsT_scale=plane[:, H * t:H * (t + 1)],
+                                        rhs=gw[:, H * h:H * (h + 1)].bitcast(E2M1X4),
+                                        rhs_scale=gs[:, H * h:H * (h + 1)], start=True, stop=True)
+                nc.scalar.copy(rounded[:, 4 * H * h:4 * H * (h + 1)].rearrange("p (j t) -> p j t", t=4),
+                               bank[:].rearrange("p t j -> p j t"))
+            return rounded
+
+        a_bf = first_stage("a", l1, w_raw, ws_raw, E4M3X4)
+        b_bf = first_stage("b", l2, w2_raw, w2s_raw, E5M2X4)
+
+        def make_kb(c, tag):
+            g = sb_tile(f"gb{c}", [P, 4, H], U8, tag)
+            for t in range(4):
+                nc.vector.tensor_copy(g[:, t, :], cb_t[t][:].indirect(l4[:, 8 * c:8 * c + 8]))
+            il = sb_tile(f"kb{c}_il", [P, H, 4], BF16)
+            for t in range(4):
+                nc.vector.tensor_scalar(il[:, :, t], g[:, t, :].bitcast(F8), sb_t[:, t:t + 1], None, MULT)
+            return il
+
+        kaq = quantize("kaq", ka_il[:], U)
+        kb0_il = make_kb(0, None)
+        aq = quantize("aq", a_bf[:], J)
+        kbq0 = quantize("kbq0", kb0_il[:].rearrange("p u t -> p (u t)"), H)
+        bq = quantize("bq", b_bf[:], J)
+
+        def score(c, kbq, copy_out):
+            for h in range(2):
+                bank = psum.tile([P, H], F32, name=f"p_bank{c}{h}")
+                js = slice(H * h, H * (h + 1))
+                us = slice(H * c, H * (c + 1))
+                nc.tensor.matmul_mx(out=bank[:], lhsT=aq[0][:, js].bitcast(E4M3X4), lhsT_scale=aq[1][:, js],
+                                    rhs=kaq[0][:, us].bitcast(E4M3X4), rhs_scale=kaq[1][:, us], start=True, stop=False)
+                nc.tensor.matmul_mx(out=bank[:], lhsT=bq[0][:, js].bitcast(E4M3X4), lhsT_scale=bq[1][:, js],
+                                    rhs=kbq[0][:].bitcast(E4M3X4), rhs_scale=kbq[1][:], start=False, stop=True)
+                rows = sb_tile(f"p{c}{h}", [P, H], F32)
+                copy_out(rows[:], bank[:])
+                nc.scalar.activation(pages[h][:].indirect(l5[:, 8 * c:8 * c + 8]), rows[:], COPY,
+                                     scale=sz_t[:, h:h + 1])
+
+        score(0, kbq0, nc.scalar.copy)
+
+        kb1_il = make_kb(1, "b_bf")
+        kbq1 = quantize("kbq1", kb1_il[:].rearrange("p u t -> p (u t)"), H)
+        score(1, kbq1, nc.vector.tensor_copy)
+        for h in range(2):
+            nc.sync.dma_start(out[H * h:H * (h + 1), :], pages[h][:])

@@ -1,6 +1,7 @@
 from contextlib import ExitStack
 
 import concourse.mybir as mybir
+from concourse.masks import make_identity
 
 K, T, J, R, V, U, E = 512, 2048, 256, 512, 1024, 256, 512
 FLOPS = 2 * (2 * K * R * J) + 2 * (2 * R * J * U)
@@ -51,44 +52,51 @@ def tile_list_scoredboth_kernel(tc, xt_words, xt_scales, w_words, w_scales, w2_w
             for q in range(4):
                 queue.dma_start(plane[32 * q:32 * q + 4, :].bitcast(I32), src[0, 4 * q:4 * q + 4, :].bitcast(I32))
 
+        def load_rows(name, src):
+            tile = sb_tile(name, [4, 4, R // 4], I32)
+            nc.sync.dma_start(tile[:], src[0].bitcast(I32).rearrange("(q r) c -> r q c", q=4))
+            return tile
+
         def load_words(name, src):
             tile = sb_tile(name, [P, R], U32)
             nc.sync.dma_start(tile[:].bitcast(I32), src[0].rearrange("p n t -> p (n t)").bitcast(I32))
             return tile
 
-        xs = cleared_plane(nc.gpsimd, "xs", T)
-        ws_raw = cleared_plane(nc.vector, "ws_raw", R)
-        w2s_raw = cleared_plane(nc.vector, "w2s_raw", R)
+        xs = cleared_plane(nc.vector, "xs", T)
+        ws = cleared_plane(nc.vector, "ws", R)
+        w2s = cleared_plane(nc.vector, "w2s", R)
         pages = [sb_tile(f"page{h}", [P, E], F32) for h in range(2)]
         for h in range(2):
             nc.vector.memset(pages[h][:], 0.0)
 
         sb_t = sb_tile("sb_t", [P, 4], F32)
         nc.gpsimd.dma_start(sb_t[:], sb.rearrange("(p t) o -> p (t o)", t=4))
-        sz_t = sb_tile("sz_t", [P, 2], F32)
-        with nc.allow_non_contiguous_dma(reason="one weight a partition"):
-            nc.gpsimd.dma_start(sz_t[:], sz.rearrange("(h p) o -> p (h o)", h=2))
+        ident = sb_tile("ident", [P, P], F32)
+        make_identity(nc, ident[:])
 
         l3 = load_list("l3", offs3)
         ca_t = [load_table("ca0", ca, 0)]
         sa_t = sb_tile("sa_t", [P, 4], F32)
         nc.sync.dma_start(sa_t[:], sa.rearrange("(p t) o -> p (t o)", t=4))
+        l1 = load_list("l1", offs)
         ca_t.extend(load_table(f"ca{t}", ca, t) for t in range(1, 4))
         xw = sb_tile("xw", [P, T], U16)
         nc.sync.dma_start(xw[:].bitcast(I32), xt_words[0].bitcast(I32))
-        l1 = load_list("l1", offs)
+        l2 = load_list("l2", offs2)
         load_plane(nc.sync, xs, xt_scales)
         w_raw = load_words("w_raw", w_words)
-        load_plane(nc.sync, ws_raw, w_scales)
-        l2 = load_list("l2", offs2)
+        ws_rows = load_rows("ws_rows", w_scales)
         w2_raw = load_words("w2_raw", w2_words)
-        load_plane(nc.sync, w2s_raw, w2_scales)
+        w2s_rows = load_rows("w2s_rows", w2_scales)
         l4 = load_list("l4", offs4)
         cb_t = [load_table(f"cb{t}", cb, t) for t in range(4)]
         l5 = load_list("l5", offs5)
+        sz_t = sb_tile("sz_t", [P, 2], F32)
+        with nc.allow_non_contiguous_dma(reason="one weight a partition"):
+            nc.sync.dma_start(sz_t[:], sz.rearrange("(h p) o -> p (h o)", h=2))
 
-        def quantize(name, src, n):
-            words = sb_tile(name + "_w", [P, n], U32)
+        def quantize(name, src, n, tag=None):
+            words = sb_tile(name + "_w", [P, n], U32, tag)
             scales = sb_tile(name + "_s", [P, n], U8)
             nc.vector.quantize_mx(out=words[:].bitcast(E4M3X4), scales=scales[:], in_=src)
             return words, scales
@@ -105,66 +113,70 @@ def tile_list_scoredboth_kernel(tc, xt_words, xt_scales, w_words, w_scales, w2_w
         ka_il = sb_tile("ka_il", [P, 4 * U], BF16)
         interleave(nc.scalar.copy, ka_il, ka_rows)
 
-        def first_stage(name, lst, raw_words, raw_plane, fmt):
-            gw = sb_tile(name + "_gw", [P, J], U16)
+        def first_stage(name, lst, words, rows, plane, fmt, gw_tag, gs_tag):
+            gw = sb_tile(name + "_gw", [P, J], U16, gw_tag)
             nc.vector.tensor_copy(gw[:], xw[:].indirect(lst[:]))
-            gs = sb_tile(name + "_gs", [P, J], U8)
+            gs = sb_tile(name + "_gs", [P, J], U8, gs_tag)
             nc.vector.tensor_copy(gs[:], xs[:].indirect(lst[:]))
-            words = sb_tile(name + "_words", [P, R], U32)
-            nc.scalar.copy(words[:].rearrange("p (t c i) -> p c t i", t=4, i=4),
-                           raw_words[:].rearrange("p (c i t) -> p c t i", t=4, i=4))
-            plane = sb_tile(name + "_plane", [P, R], U8)
-            nc.vector.tensor_copy(plane[:].rearrange("p (t m) -> p t m", t=4),
-                                  raw_plane[:].rearrange("p (m t) -> p t m", t=4))
-            rounded = sb_tile(name + "_bf", [P, 4 * J], BF16)
+            for q in range(4):
+                nc.vector.tensor_copy(plane[32 * q:32 * q + 4, :].bitcast(I32), rows[:, q, :])
+            turned = psum.tile([P, 2, 2, H], F32, name=name + "_turned")
             for h in range(2):
-                bank = psum.tile([P, 4, H], F32, name=f"{name}_bank{h}")
-                for t in range(4):
-                    nc.tensor.matmul_mx(out=bank[:, t, :],
-                                        lhsT=words[:, H * t:H * (t + 1)].bitcast(fmt),
-                                        lhsT_scale=plane[:, H * t:H * (t + 1)],
-                                        rhs=gw[:, H * h:H * (h + 1)].bitcast(E2M1X4),
-                                        rhs_scale=gs[:, H * h:H * (h + 1)], start=True, stop=True)
-                nc.scalar.copy(rounded[:, 4 * H * h:4 * H * (h + 1)].rearrange("p (j t) -> p j t", t=4),
-                               bank[:].rearrange("p t j -> p j t"))
+                bank = psum.tile([P, R], F32, name=f"{name}_bank{h}")
+                nc.tensor.matmul_mx(out=bank[:], lhsT=gw[:, H * h:H * (h + 1)].bitcast(E2M1X4),
+                                    lhsT_scale=gs[:, H * h:H * (h + 1)],
+                                    rhs=words[:].bitcast(fmt), rhs_scale=plane[:], start=True, stop=True)
+                by_slot = sb_tile(f"{name}_by_slot{h}", [P, R], BF16)
+                nc.scalar.copy(by_slot[:].rearrange("j (u p e) -> j u p e", u=2, e=2),
+                               bank[:].rearrange("j (p u e) -> j u p e", u=2, e=2))
+                for u in range(2):
+                    nc.tensor.transpose(turned[:, h, u, :], by_slot[:].bitcast(F32)[:, P * u:P * (u + 1)], ident[:])
+            return turned
+
+        def take_back(name, turned):
+            rounded = sb_tile(name + "_bf", [P, 4 * J], BF16)
+            nc.scalar.copy(rounded[:].bitcast(F32).rearrange("p (h j u) -> p h j u", h=2, u=2),
+                           turned[:].rearrange("p h u j -> p h j u"))
             return rounded
 
-        a_bf = first_stage("a", l1, w_raw, ws_raw, E4M3X4)
-        b_bf = first_stage("b", l2, w2_raw, w2s_raw, E5M2X4)
+        a_bf = take_back("a", first_stage("a", l1, w_raw, ws_rows, ws, E4M3X4, None, None))
+        b_turned = first_stage("b", l2, w2_raw, w2s_rows, w2s, E5M2X4, "a_gs", "ws_rows")
+
+        kaq = quantize("kaq", ka_il[:], U, "xs")
+
+        gb = sb_tile("gb", [P, 8 * H], U8, "xw")
+        for c in range(2):
+            for t in range(4):
+                at = H * (4 * c + t)
+                nc.vector.tensor_copy(gb[:, at:at + H], cb_t[t][:].indirect(l4[:, 8 * c:8 * c + 8]))
 
         def make_kb(c, tag):
-            g = sb_tile(f"gb{c}", [P, 4, H], U8, tag)
+            rows = sb_tile(f"kb{c}_rows", [P, 4, H], BF16, tag)
             for t in range(4):
-                nc.vector.tensor_copy(g[:, t, :], cb_t[t][:].indirect(l4[:, 8 * c:8 * c + 8]))
-            il = sb_tile(f"kb{c}_il", [P, H, 4], BF16)
-            for t in range(4):
-                nc.vector.tensor_scalar(il[:, :, t], g[:, t, :].bitcast(F8), sb_t[:, t:t + 1], None, MULT)
-            return il
+                at = H * (4 * c + t)
+                nc.scalar.activation(rows[:, t, :], gb[:, at:at + H].bitcast(F8), COPY, scale=sb_t[:, t:t + 1])
+            il = sb_tile(f"kb{c}_il", [P, 4 * H], BF16)
+            interleave(nc.vector.tensor_copy, il, rows)
+            return quantize(f"kbq{c}", il[:], H)
 
-        kaq = quantize("kaq", ka_il[:], U)
-        kb0_il = make_kb(0, None)
         aq = quantize("aq", a_bf[:], J)
-        kbq0 = quantize("kbq0", kb0_il[:].rearrange("p u t -> p (u t)"), H)
-        bq = quantize("bq", b_bf[:], J)
+        kbq = make_kb(0, "a_gs")
+        bq = quantize("bq", take_back("b", b_turned)[:], J)
 
-        def score(c, kbq, copy_out):
+        for c in range(2):
+            if c == 1:
+                kbq = make_kb(1, "b_by_slot1")
             for h in range(2):
-                bank = psum.tile([P, H], F32, name=f"p_bank{c}{h}")
+                bank = psum.tile([P, H], F32, name=f"p_bank{c}{h}", tag=f"a_bank{h}" if c == 0 else f"p_bank{h}")
                 js = slice(H * h, H * (h + 1))
                 us = slice(H * c, H * (c + 1))
-                nc.tensor.matmul_mx(out=bank[:], lhsT=aq[0][:, js].bitcast(E4M3X4), lhsT_scale=aq[1][:, js],
-                                    rhs=kaq[0][:, us].bitcast(E4M3X4), rhs_scale=kaq[1][:, us], start=True, stop=False)
                 nc.tensor.matmul_mx(out=bank[:], lhsT=bq[0][:, js].bitcast(E4M3X4), lhsT_scale=bq[1][:, js],
-                                    rhs=kbq[0][:].bitcast(E4M3X4), rhs_scale=kbq[1][:], start=False, stop=True)
+                                    rhs=kbq[0][:].bitcast(E4M3X4), rhs_scale=kbq[1][:], start=True, stop=False)
+                nc.tensor.matmul_mx(out=bank[:], lhsT=aq[0][:, js].bitcast(E4M3X4), lhsT_scale=aq[1][:, js],
+                                    rhs=kaq[0][:, us].bitcast(E4M3X4), rhs_scale=kaq[1][:, us], start=False, stop=True)
                 rows = sb_tile(f"p{c}{h}", [P, H], F32)
-                copy_out(rows[:], bank[:])
+                nc.vector.tensor_copy(rows[:], bank[:])
                 nc.scalar.activation(pages[h][:].indirect(l5[:, 8 * c:8 * c + 8]), rows[:], COPY,
                                      scale=sz_t[:, h:h + 1])
-
-        score(0, kbq0, nc.scalar.copy)
-
-        kb1_il = make_kb(1, "b_bf")
-        kbq1 = quantize("kbq1", kb1_il[:].rearrange("p u t -> p (u t)"), H)
-        score(1, kbq1, nc.vector.tensor_copy)
         for h in range(2):
             nc.sync.dma_start(out[H * h:H * (h + 1), :], pages[h][:])

@@ -48,9 +48,9 @@ def tile_list_scoredboth_kernel(tc, xt_words, xt_scales, w_words, w_scales, w2_w
             engine.memset(tile[:].bitcast(I32), 0)
             return tile
 
-        def load_plane(queue, plane, src):
-            for q in range(4):
-                queue.dma_start(plane[32 * q:32 * q + 4, :].bitcast(I32), src[0, 4 * q:4 * q + 4, :].bitcast(I32))
+        def load_plane(queue, plane, src, rows):
+            for r in rows:
+                queue.dma_start(plane[r:P:32, :].bitcast(I32), src[0, r:16:4, :].bitcast(I32))
 
         def load_rows(name, src):
             tile = sb_tile(name, [4, 4, R // 4], I32)
@@ -62,15 +62,14 @@ def tile_list_scoredboth_kernel(tc, xt_words, xt_scales, w_words, w_scales, w2_w
             nc.sync.dma_start(tile[:].bitcast(I32), src[0].rearrange("p n t -> p (n t)").bitcast(I32))
             return tile
 
-        xs = cleared_plane(nc.vector, "xs", T)
+        xs = cleared_plane(nc.gpsimd, "xs", T)
         ws = cleared_plane(nc.vector, "ws", R)
         w2s = cleared_plane(nc.vector, "w2s", R)
         pages = [sb_tile(f"page{h}", [P, E], F32) for h in range(2)]
         for h in range(2):
             nc.vector.memset(pages[h][:], 0.0)
 
-        sb_t = sb_tile("sb_t", [P, 4], F32)
-        nc.gpsimd.dma_start(sb_t[:], sb.rearrange("(p t) o -> p (t o)", t=4))
+        load_plane(nc.gpsimd, xs, xt_scales, (0, 1))
         ident = sb_tile("ident", [P, P], F32)
         make_identity(nc, ident[:])
 
@@ -83,13 +82,15 @@ def tile_list_scoredboth_kernel(tc, xt_words, xt_scales, w_words, w_scales, w2_w
         xw = sb_tile("xw", [P, T], U16)
         nc.sync.dma_start(xw[:].bitcast(I32), xt_words[0].bitcast(I32))
         l2 = load_list("l2", offs2)
-        load_plane(nc.sync, xs, xt_scales)
+        load_plane(nc.sync, xs, xt_scales, (2, 3))
         w_raw = load_words("w_raw", w_words)
         ws_rows = load_rows("ws_rows", w_scales)
         w2_raw = load_words("w2_raw", w2_words)
         w2s_rows = load_rows("w2s_rows", w2_scales)
         l4 = load_list("l4", offs4)
         cb_t = [load_table(f"cb{t}", cb, t) for t in range(4)]
+        sb_t = sb_tile("sb_t", [P, 4], F32)
+        nc.sync.dma_start(sb_t[:], sb.rearrange("(p t) o -> p (t o)", t=4))
         l5 = load_list("l5", offs5)
         sz_t = sb_tile("sz_t", [P, 2], F32)
         with nc.allow_non_contiguous_dma(reason="one weight a partition"):
@@ -150,22 +151,22 @@ def tile_list_scoredboth_kernel(tc, xt_words, xt_scales, w_words, w_scales, w2_w
                 at = H * (4 * c + t)
                 nc.vector.tensor_copy(gb[:, at:at + H], cb_t[t][:].indirect(l4[:, 8 * c:8 * c + 8]))
 
-        def make_kb(c, tag):
+        def make_kb(c, tag, il_tag):
             rows = sb_tile(f"kb{c}_rows", [P, 4, H], BF16, tag)
             for t in range(4):
                 at = H * (4 * c + t)
                 nc.scalar.activation(rows[:, t, :], gb[:, at:at + H].bitcast(F8), COPY, scale=sb_t[:, t:t + 1])
-            il = sb_tile(f"kb{c}_il", [P, 4 * H], BF16)
+            il = sb_tile(f"kb{c}_il", [P, 4 * H], BF16, il_tag)
             interleave(nc.vector.tensor_copy, il, rows)
             return quantize(f"kbq{c}", il[:], H)
 
         aq = quantize("aq", a_bf[:], J)
-        kbq = make_kb(0, "a_gs")
+        kbq = make_kb(0, "a_gs", None)
         bq = quantize("bq", take_back("b", b_turned)[:], J)
 
         for c in range(2):
             if c == 1:
-                kbq = make_kb(1, "b_by_slot1")
+                kbq = make_kb(1, "b_by_slot1", "b_bf")
             for h in range(2):
                 bank = psum.tile([P, H], F32, name=f"p_bank{c}{h}", tag=f"a_bank{h}" if c == 0 else f"p_bank{h}")
                 js = slice(H * h, H * (h + 1))
@@ -175,7 +176,7 @@ def tile_list_scoredboth_kernel(tc, xt_words, xt_scales, w_words, w_scales, w2_w
                 nc.tensor.matmul_mx(out=bank[:], lhsT=aq[0][:, js].bitcast(E4M3X4), lhsT_scale=aq[1][:, js],
                                     rhs=kaq[0][:, us].bitcast(E4M3X4), rhs_scale=kaq[1][:, us], start=False, stop=True)
                 rows = sb_tile(f"p{c}{h}", [P, H], F32)
-                nc.vector.tensor_copy(rows[:], bank[:])
+                (nc.scalar.copy if c == 0 else nc.vector.tensor_copy)(rows[:], bank[:])
                 nc.scalar.activation(pages[h][:].indirect(l5[:, 8 * c:8 * c + 8]), rows[:], COPY,
                                      scale=sz_t[:, h:h + 1])
         for h in range(2):

@@ -1,7 +1,6 @@
 from contextlib import ExitStack
 
 import concourse.mybir as mybir
-from concourse.masks import make_identity
 
 K, T, J, R, V, U, E = 512, 2048, 256, 512, 1024, 256, 512
 FLOPS = 2 * (2 * K * R * J) + 2 * (2 * R * J * U)
@@ -17,10 +16,13 @@ E4M3X4 = mybir.dt.float8_e4m3fn_x4
 E5M2X4 = mybir.dt.float8_e5m2_x4
 E2M1X4 = mybir.dt.float4_e2m1fn_x4
 COPY = mybir.ActivationFunctionType.Copy
-MULT = mybir.AluOpType.mult
 
 P = 128
-H = 128
+PACK = 4
+HALF = 128
+QUADRANT = 32
+GROUP = 16
+RUN = 4
 
 
 def tile_list_scoredboth_kernel(tc, xt_words, xt_scales, w_words, w_scales, w2_words, w2_scales,
@@ -30,154 +32,152 @@ def tile_list_scoredboth_kernel(tc, xt_words, xt_scales, w_words, w_scales, w2_w
         pool = ctx.enter_context(tc.tile_pool(name="held", bufs=1))
         psum = ctx.enter_context(tc.psum_pool(name="psum", bufs=1))
 
-        def sb_tile(name, shape, dtype, tag=None):
-            return pool.tile(shape, dtype, name=name, tag=tag or name, align_bytes=64)
+        def sb_tile(name, shape, dtype, reuse=None):
+            return pool.tile(shape, dtype, name=name, tag=reuse or name, align_bytes=64)
 
         def load_list(name, src):
-            tile = sb_tile(name, [P, 16], U16)
+            tile = sb_tile(name, [P, J // GROUP], U16)
             nc.sync.dma_start(tile[:], src)
             return tile
 
-        def load_table(name, src, t):
+        def load_key_slice(name, src, t):
             tile = sb_tile(name, [P, V], U8)
-            nc.sync.dma_start(tile[:], src.rearrange("(p t) v -> p t v", t=4)[:, t, :])
+            nc.sync.dma_start(tile[:], src.rearrange("(q t) v -> q t v", t=PACK)[:, t, :])
             return tile
 
-        def cleared_plane(engine, name, width):
+        def load_steps(queue, name, src):
+            tile = sb_tile(name, [P, PACK], F32)
+            queue.dma_start(tile[:], src.rearrange("(q t) o -> q (t o)", t=PACK))
+            return tile
+
+        def cleared_plane(name, width):
             tile = sb_tile(name, [P, width], U8)
-            engine.memset(tile[:].bitcast(I32), 0)
+            nc.vector.memset(tile[:].bitcast(I32), 0)
             return tile
 
-        def load_plane(queue, plane, src, rows):
-            for r in rows:
-                queue.dma_start(plane[r:P:32, :].bitcast(I32), src[0, r:16:4, :].bitcast(I32))
-
-        def load_rows(name, src):
-            tile = sb_tile(name, [4, 4, R // 4], I32)
-            nc.sync.dma_start(tile[:], src[0].bitcast(I32).rearrange("(q r) c -> r q c", q=4))
+        def load_scale_rows(name, src):
+            tile = sb_tile(name, [PACK, PACK, R // 4], I32)
+            nc.sync.dma_start(tile[:], src[0].bitcast(I32).rearrange("(Q i) c -> i Q c", Q=PACK))
             return tile
 
         def load_words(name, src):
             tile = sb_tile(name, [P, R], U32)
-            nc.sync.dma_start(tile[:].bitcast(I32), src[0].rearrange("p n t -> p (n t)").bitcast(I32))
+            nc.sync.dma_start(tile[:].bitcast(I32), src[0].rearrange("q n t -> q (n t)").bitcast(I32))
             return tile
 
-        xs = cleared_plane(nc.gpsimd, "xs", T)
-        ws = cleared_plane(nc.vector, "ws", R)
-        w2s = cleared_plane(nc.vector, "w2s", R)
+        xs = cleared_plane("xs", T)
+        ws = cleared_plane("ws", R)
+        w2s = cleared_plane("w2s", R)
         pages = [sb_tile(f"page{h}", [P, E], F32) for h in range(2)]
         for h in range(2):
             nc.vector.memset(pages[h][:], 0.0)
 
-        load_plane(nc.gpsimd, xs, xt_scales, (0, 1))
-        ident = sb_tile("ident", [P, P], F32)
-        make_identity(nc, ident[:])
+        sb_t = load_steps(nc.gpsimd, "sb_t", sb)
 
         l3 = load_list("l3", offs3)
-        ca_t = [load_table("ca0", ca, 0)]
-        sa_t = sb_tile("sa_t", [P, 4], F32)
-        nc.sync.dma_start(sa_t[:], sa.rearrange("(p t) o -> p (t o)", t=4))
+        ca_t = [load_key_slice("ca0", ca, 0)]
+        sa_t = load_steps(nc.sync, "sa_t", sa)
         l1 = load_list("l1", offs)
-        ca_t.extend(load_table(f"ca{t}", ca, t) for t in range(1, 4))
+        ca_t.extend(load_key_slice(f"ca{t}", ca, t) for t in range(1, PACK))
         xw = sb_tile("xw", [P, T], U16)
         nc.sync.dma_start(xw[:].bitcast(I32), xt_words[0].bitcast(I32))
         l2 = load_list("l2", offs2)
-        load_plane(nc.sync, xs, xt_scales, (2, 3))
+        for Q in range(PACK):
+            nc.sync.dma_start(xs[QUADRANT * Q:QUADRANT * Q + PACK, :].bitcast(I32),
+                              xt_scales[0, PACK * Q:PACK * (Q + 1), :].bitcast(I32))
         w_raw = load_words("w_raw", w_words)
-        ws_rows = load_rows("ws_rows", w_scales)
+        ws_rows = load_scale_rows("ws_rows", w_scales)
         w2_raw = load_words("w2_raw", w2_words)
-        w2s_rows = load_rows("w2s_rows", w2_scales)
+        w2s_rows = load_scale_rows("w2s_rows", w2_scales)
         l4 = load_list("l4", offs4)
-        cb_t = [load_table(f"cb{t}", cb, t) for t in range(4)]
-        sb_t = sb_tile("sb_t", [P, 4], F32)
-        nc.sync.dma_start(sb_t[:], sb.rearrange("(p t) o -> p (t o)", t=4))
+        cb_t = [load_key_slice(f"cb{t}", cb, t) for t in range(PACK)]
         l5 = load_list("l5", offs5)
         sz_t = sb_tile("sz_t", [P, 2], F32)
         with nc.allow_non_contiguous_dma(reason="one weight a partition"):
-            nc.sync.dma_start(sz_t[:], sz.rearrange("(h p) o -> p (h o)", h=2))
+            nc.sync.dma_start(sz_t[:], sz.rearrange("(h q) o -> q (h o)", h=2))
 
-        def quantize(name, src, n, tag=None):
-            words = sb_tile(name + "_w", [P, n], U32, tag)
-            scales = sb_tile(name + "_s", [P, n], U8)
-            nc.vector.quantize_mx(out=words[:].bitcast(E4M3X4), scales=scales[:], in_=src)
-            return words, scales
+        def quantize(name, src, columns, reuse=None):
+            words = sb_tile(name + "_w", [P, columns], U32, reuse)
+            plane = sb_tile(name + "_s", [P, columns], U8)
+            nc.vector.quantize_mx(out=words[:].bitcast(E4M3X4), scales=plane[:], in_=src)
+            return words, plane
 
-        def interleave(engine_copy, dst, src):
-            engine_copy(dst[:].rearrange("p (c i t) -> p c t i", i=4, t=4),
-                        src[:].rearrange("p t (c i) -> p c t i", i=4))
+        ka_slices = sb_tile("ka_rows", [P, PACK, U], BF16)
+        for t in range(PACK):
+            looked_up = sb_tile(f"ga{t}", [P, U], U8)
+            nc.vector.tensor_copy(looked_up[:], ca_t[t][:].indirect(l3[:]))
+            nc.scalar.activation(ka_slices[:, t, :], looked_up[:].bitcast(F8), COPY, scale=sa_t[:, t:t + 1])
+        ka_bf = sb_tile("ka_il", [P, PACK * U], BF16)
+        nc.scalar.copy(ka_bf[:].rearrange("q (c i t) -> q c t i", i=RUN, t=PACK),
+                       ka_slices[:].rearrange("q t (c i) -> q c t i", i=RUN))
 
-        ka_rows = sb_tile("ka_rows", [P, 4, U], BF16)
-        for t in range(4):
-            g = sb_tile(f"ga{t}", [P, U], U8)
-            nc.vector.tensor_copy(g[:], ca_t[t][:].indirect(l3[:]))
-            nc.scalar.activation(ka_rows[:, t, :], g[:].bitcast(F8), COPY, scale=sa_t[:, t:t + 1])
-        ka_il = sb_tile("ka_il", [P, 4 * U], BF16)
-        interleave(nc.scalar.copy, ka_il, ka_rows)
-
-        def first_stage(name, lst, words, rows, plane, fmt, gw_tag, gs_tag):
-            gw = sb_tile(name + "_gw", [P, J], U16, gw_tag)
-            nc.vector.tensor_copy(gw[:], xw[:].indirect(lst[:]))
-            gs = sb_tile(name + "_gs", [P, J], U8, gs_tag)
-            nc.vector.tensor_copy(gs[:], xs[:].indirect(lst[:]))
-            for q in range(4):
-                nc.vector.tensor_copy(plane[32 * q:32 * q + 4, :].bitcast(I32), rows[:, q, :])
-            turned = psum.tile([P, 2, 2, H], F32, name=name + "_turned")
+        def first_stage(name, tokens, raw_words, scale_rows, raw_plane, fmt, picked_plane_reuse, dealt_words_reuse):
+            picked_words = sb_tile(name + "_gw", [P, J], U16)
+            nc.vector.tensor_copy(picked_words[:], xw[:].indirect(tokens[:]))
+            picked_plane = sb_tile(name + "_gs", [P, J], U8, picked_plane_reuse)
+            nc.vector.tensor_copy(picked_plane[:], xs[:].indirect(tokens[:]))
+            for Q in range(PACK):
+                nc.vector.tensor_copy(raw_plane[QUADRANT * Q:QUADRANT * Q + PACK, :].bitcast(I32), scale_rows[:, Q, :])
+            dealt_plane = sb_tile(name + "_plane", [P, R], U8)
+            nc.vector.tensor_copy(dealt_plane[:].rearrange("q (t m) -> q t m", t=PACK),
+                                  raw_plane[:].rearrange("q (m t) -> q t m", t=PACK))
+            dealt_words = sb_tile(name + "_words", [P, R], U32, dealt_words_reuse)
+            nc.scalar.copy(dealt_words[:].rearrange("q (t c i) -> q c t i", t=PACK, i=RUN),
+                           raw_words[:].rearrange("q (c i t) -> q c t i", t=PACK, i=RUN))
+            rounded = sb_tile(name + "_bf", [P, PACK * J], BF16)
             for h in range(2):
-                bank = psum.tile([P, R], F32, name=f"{name}_bank{h}")
-                nc.tensor.matmul_mx(out=bank[:], lhsT=gw[:, H * h:H * (h + 1)].bitcast(E2M1X4),
-                                    lhsT_scale=gs[:, H * h:H * (h + 1)],
-                                    rhs=words[:].bitcast(fmt), rhs_scale=plane[:], start=True, stop=True)
-                by_slot = sb_tile(f"{name}_by_slot{h}", [P, R], BF16)
-                nc.scalar.copy(by_slot[:].rearrange("j (u p e) -> j u p e", u=2, e=2),
-                               bank[:].rearrange("j (p u e) -> j u p e", u=2, e=2))
-                for u in range(2):
-                    nc.tensor.transpose(turned[:, h, u, :], by_slot[:].bitcast(F32)[:, P * u:P * (u + 1)], ident[:])
-            return turned
-
-        def take_back(name, turned):
-            rounded = sb_tile(name + "_bf", [P, 4 * J], BF16)
-            nc.scalar.copy(rounded[:].bitcast(F32).rearrange("p (h j u) -> p h j u", h=2, u=2),
-                           turned[:].rearrange("p h u j -> p h j u"))
+                slots = slice(HALF * h, HALF * (h + 1))
+                bank = psum.tile([P, PACK, HALF], F32, name=f"{name}_bank{h}")
+                for t in range(PACK):
+                    nc.tensor.matmul_mx(out=bank[:, t, :],
+                                        lhsT=dealt_words[:, P * t:P * (t + 1)].bitcast(fmt),
+                                        lhsT_scale=dealt_plane[:, P * t:P * (t + 1)],
+                                        rhs=picked_words[:, slots].bitcast(E2M1X4),
+                                        rhs_scale=picked_plane[:, slots], start=True, stop=True)
+                nc.scalar.copy(rounded[:, PACK * HALF * h:PACK * HALF * (h + 1)].rearrange("q (j t) -> q j t", t=PACK),
+                               bank[:].rearrange("q t j -> q j t"))
             return rounded
 
-        a_bf = take_back("a", first_stage("a", l1, w_raw, ws_rows, ws, E4M3X4, None, None))
-        b_turned = first_stage("b", l2, w2_raw, w2s_rows, w2s, E5M2X4, "a_gs", "ws_rows")
+        a_bf = first_stage("a", l1, w_raw, ws_rows, ws, E4M3X4, None, "ka_rows")
+        b_bf = first_stage("b", l2, w2_raw, w2s_rows, w2s, E5M2X4, "ws", "w_raw")
 
-        kaq = quantize("kaq", ka_il[:], U, "xs")
+        ka_words, ka_plane = quantize("kaq", ka_bf[:], U, "xs")
 
-        gb = sb_tile("gb", [P, 8 * H], U8, "xw")
+        kb_bytes = sb_tile("gb", [P, PACK * U], U8, "w2s")
+        kb_slices = sb_tile("kb_rows", [P, PACK * U], BF16, "b_gw")
+        entries = [slice(HALF // GROUP * c, HALF // GROUP * (c + 1)) for c in range(2)]
         for c in range(2):
-            for t in range(4):
-                at = H * (4 * c + t)
-                nc.vector.tensor_copy(gb[:, at:at + H], cb_t[t][:].indirect(l4[:, 8 * c:8 * c + 8]))
+            for t in range(PACK):
+                at = slice(HALF * (PACK * c + t), HALF * (PACK * c + t + 1))
+                nc.vector.tensor_copy(kb_bytes[:, at], cb_t[t][:].indirect(l4[:, entries[c]]))
+                nc.scalar.activation(kb_slices[:, at], kb_bytes[:, at].bitcast(F8), COPY, scale=sb_t[:, t:t + 1])
 
-        def make_kb(c, tag, il_tag):
-            rows = sb_tile(f"kb{c}_rows", [P, 4, H], BF16, tag)
-            for t in range(4):
-                at = H * (4 * c + t)
-                nc.scalar.activation(rows[:, t, :], gb[:, at:at + H].bitcast(F8), COPY, scale=sb_t[:, t:t + 1])
-            il = sb_tile(f"kb{c}_il", [P, 4 * H], BF16, il_tag)
-            interleave(nc.vector.tensor_copy, il, rows)
-            return quantize(f"kbq{c}", il[:], H)
+        def quantize_kb(c):
+            kb_bf = sb_tile(f"kb{c}_il", [P, PACK * HALF], BF16, "kb0_il")
+            half = kb_slices[:, PACK * HALF * c:PACK * HALF * (c + 1)]
+            nc.vector.tensor_copy(kb_bf[:].rearrange("q (c i t) -> q c t i", i=RUN, t=PACK),
+                                  half.rearrange("q (t c i) -> q c t i", t=PACK, i=RUN))
+            return quantize(f"kbq{c}", kb_bf[:], HALF)
 
-        aq = quantize("aq", a_bf[:], J)
-        kbq = make_kb(0, "a_gs", None)
-        bq = quantize("bq", take_back("b", b_turned)[:], J)
-
-        for c in range(2):
-            if c == 1:
-                kbq = make_kb(1, "b_by_slot1", "b_bf")
+        def score_and_put(c, kb_words, kb_plane, copy_out):
+            candidates = slice(HALF * c, HALF * (c + 1))
             for h in range(2):
-                bank = psum.tile([P, H], F32, name=f"p_bank{c}{h}", tag=f"a_bank{h}" if c == 0 else f"p_bank{h}")
-                js = slice(H * h, H * (h + 1))
-                us = slice(H * c, H * (c + 1))
-                nc.tensor.matmul_mx(out=bank[:], lhsT=bq[0][:, js].bitcast(E4M3X4), lhsT_scale=bq[1][:, js],
-                                    rhs=kbq[0][:].bitcast(E4M3X4), rhs_scale=kbq[1][:], start=True, stop=False)
-                nc.tensor.matmul_mx(out=bank[:], lhsT=aq[0][:, js].bitcast(E4M3X4), lhsT_scale=aq[1][:, js],
-                                    rhs=kaq[0][:, us].bitcast(E4M3X4), rhs_scale=kaq[1][:, us], start=False, stop=True)
-                rows = sb_tile(f"p{c}{h}", [P, H], F32)
-                (nc.scalar.copy if c == 0 else nc.vector.tensor_copy)(rows[:], bank[:])
-                nc.scalar.activation(pages[h][:].indirect(l5[:, 8 * c:8 * c + 8]), rows[:], COPY,
-                                     scale=sz_t[:, h:h + 1])
+                slots = slice(HALF * h, HALF * (h + 1))
+                bank = psum.tile([P, HALF], F32, name=f"p_bank{c}{h}")
+                nc.tensor.matmul_mx(out=bank[:], lhsT=b_words[:, slots].bitcast(E4M3X4), lhsT_scale=b_plane[:, slots],
+                                    rhs=kb_words[:].bitcast(E4M3X4), rhs_scale=kb_plane[:], start=True, stop=False)
+                nc.tensor.matmul_mx(out=bank[:], lhsT=a_words[:, slots].bitcast(E4M3X4), lhsT_scale=a_plane[:, slots],
+                                    rhs=ka_words[:, candidates].bitcast(E4M3X4), rhs_scale=ka_plane[:, candidates],
+                                    start=False, stop=True)
+                scores = sb_tile(f"p{c}{h}", [P, HALF], F32)
+                copy_out(scores[:], bank[:])
+                nc.scalar.activation(pages[h][:].indirect(l5[:, entries[c]]), scores[:], COPY, scale=sz_t[:, h:h + 1])
+
+        a_words, a_plane = quantize("aq", a_bf[:], J)
+        first_kb = quantize_kb(0)
+        b_words, b_plane = quantize("bq", b_bf[:], J)
+
+        score_and_put(0, *first_kb, nc.scalar.copy)
+        score_and_put(1, *quantize_kb(1), nc.vector.tensor_copy)
         for h in range(2):
-            nc.sync.dma_start(out[H * h:H * (h + 1), :], pages[h][:])
+            nc.sync.dma_start(out[HALF * h:HALF * (h + 1), :], pages[h][:])

from contextlib import ExitStack

import concourse.mybir as mybir

K, T, J, R, V, U, E = 512, 2048, 256, 512, 1024, 256, 512
FLOPS = 2 * (2 * K * R * J) + 2 * (2 * R * J * U)

F32 = mybir.dt.float32
BF16 = mybir.dt.bfloat16
I32 = mybir.dt.int32
U32 = mybir.dt.uint32
U16 = mybir.dt.uint16
U8 = mybir.dt.uint8
F8 = mybir.dt.float8_e4m3fn
E4M3X4 = mybir.dt.float8_e4m3fn_x4
E5M2X4 = mybir.dt.float8_e5m2_x4
E2M1X4 = mybir.dt.float4_e2m1fn_x4
COPY = mybir.ActivationFunctionType.Copy

P = 128
PACK = 4
HALF = 128
QUADRANT = 32
GROUP = 16
RUN = 4


def tile_list_scoredboth_kernel(tc, xt_words, xt_scales, w_words, w_scales, w2_words, w2_scales,
                                   ca, cb, sa, sb, sz, offs, offs2, offs3, offs4, offs5, out):
    nc = tc.nc
    with ExitStack() as ctx:
        pool = ctx.enter_context(tc.tile_pool(name="held", bufs=1))
        psum = ctx.enter_context(tc.psum_pool(name="psum", bufs=1))

        def sb_tile(name, shape, dtype, reuse=None):
            return pool.tile(shape, dtype, name=name, tag=reuse or name, align_bytes=64)

        def load_list(name, src):
            tile = sb_tile(name, [P, J // GROUP], U16)
            nc.sync.dma_start(tile[:], src)
            return tile

        def load_key_slice(name, src, t):
            tile = sb_tile(name, [P, V], U8)
            nc.sync.dma_start(tile[:], src.rearrange("(q t) v -> q t v", t=PACK)[:, t, :])
            return tile

        def load_steps(queue, name, src):
            tile = sb_tile(name, [P, PACK], F32)
            queue.dma_start(tile[:], src.rearrange("(q t) o -> q (t o)", t=PACK))
            return tile

        def cleared_plane(name, width):
            tile = sb_tile(name, [P, width], U8)
            nc.vector.memset(tile[:].bitcast(I32), 0)
            return tile

        def load_scale_rows(name, src):
            tile = sb_tile(name, [PACK, PACK, R // 4], I32)
            nc.sync.dma_start(tile[:], src[0].bitcast(I32).rearrange("(Q i) c -> i Q c", Q=PACK))
            return tile

        def load_words(name, src):
            tile = sb_tile(name, [P, R], U32)
            nc.sync.dma_start(tile[:].bitcast(I32), src[0].rearrange("q n t -> q (n t)").bitcast(I32))
            return tile

        xs = cleared_plane("xs", T)
        ws = cleared_plane("ws", R)
        w2s = cleared_plane("w2s", R)
        pages = [sb_tile(f"page{h}", [P, E], F32) for h in range(2)]
        for h in range(2):
            nc.vector.memset(pages[h][:], 0.0)

        sb_t = load_steps(nc.gpsimd, "sb_t", sb)

        l3 = load_list("l3", offs3)
        ca_t = [load_key_slice("ca0", ca, 0)]
        sa_t = load_steps(nc.sync, "sa_t", sa)
        l1 = load_list("l1", offs)
        ca_t.extend(load_key_slice(f"ca{t}", ca, t) for t in range(1, PACK))
        xw = sb_tile("xw", [P, T], U16)
        nc.sync.dma_start(xw[:].bitcast(I32), xt_words[0].bitcast(I32))
        l2 = load_list("l2", offs2)
        for Q in range(PACK):
            nc.sync.dma_start(xs[QUADRANT * Q:QUADRANT * Q + PACK, :].bitcast(I32),
                              xt_scales[0, PACK * Q:PACK * (Q + 1), :].bitcast(I32))
        w_raw = load_words("w_raw", w_words)
        ws_rows = load_scale_rows("ws_rows", w_scales)
        w2_raw = load_words("w2_raw", w2_words)
        w2s_rows = load_scale_rows("w2s_rows", w2_scales)
        l4 = load_list("l4", offs4)
        cb_t = [load_key_slice(f"cb{t}", cb, t) for t in range(PACK)]
        l5 = load_list("l5", offs5)
        sz_t = sb_tile("sz_t", [P, 2], F32)
        with nc.allow_non_contiguous_dma(reason="one weight a partition"):
            nc.sync.dma_start(sz_t[:], sz.rearrange("(h q) o -> q (h o)", h=2))

        def quantize(name, src, columns, reuse=None):
            words = sb_tile(name + "_w", [P, columns], U32, reuse)
            plane = sb_tile(name + "_s", [P, columns], U8)
            nc.vector.quantize_mx(out=words[:].bitcast(E4M3X4), scales=plane[:], in_=src)
            return words, plane

        ka_slices = sb_tile("ka_rows", [P, PACK, U], BF16)
        for t in range(PACK):
            looked_up = sb_tile(f"ga{t}", [P, U], U8)
            nc.vector.tensor_copy(looked_up[:], ca_t[t][:].indirect(l3[:]))
            nc.scalar.activation(ka_slices[:, t, :], looked_up[:].bitcast(F8), COPY, scale=sa_t[:, t:t + 1])
        ka_bf = sb_tile("ka_il", [P, PACK * U], BF16)
        nc.scalar.copy(ka_bf[:].rearrange("q (c i t) -> q c t i", i=RUN, t=PACK),
                       ka_slices[:].rearrange("q t (c i) -> q c t i", i=RUN))

        def first_stage(name, tokens, raw_words, scale_rows, raw_plane, fmt, picked_plane_reuse, dealt_words_reuse):
            picked_words = sb_tile(name + "_gw", [P, J], U16)
            nc.vector.tensor_copy(picked_words[:], xw[:].indirect(tokens[:]))
            picked_plane = sb_tile(name + "_gs", [P, J], U8, picked_plane_reuse)
            nc.vector.tensor_copy(picked_plane[:], xs[:].indirect(tokens[:]))
            for Q in range(PACK):
                nc.vector.tensor_copy(raw_plane[QUADRANT * Q:QUADRANT * Q + PACK, :].bitcast(I32), scale_rows[:, Q, :])
            dealt_plane = sb_tile(name + "_plane", [P, R], U8)
            nc.vector.tensor_copy(dealt_plane[:].rearrange("q (t m) -> q t m", t=PACK),
                                  raw_plane[:].rearrange("q (m t) -> q t m", t=PACK))
            dealt_words = sb_tile(name + "_words", [P, R], U32, dealt_words_reuse)
            nc.scalar.copy(dealt_words[:].rearrange("q (t c i) -> q c t i", t=PACK, i=RUN),
                           raw_words[:].rearrange("q (c i t) -> q c t i", t=PACK, i=RUN))
            rounded = sb_tile(name + "_bf", [P, PACK * J], BF16)
            for h in range(2):
                slots = slice(HALF * h, HALF * (h + 1))
                bank = psum.tile([P, PACK, HALF], F32, name=f"{name}_bank{h}")
                for t in range(PACK):
                    nc.tensor.matmul_mx(out=bank[:, t, :],
                                        lhsT=dealt_words[:, P * t:P * (t + 1)].bitcast(fmt),
                                        lhsT_scale=dealt_plane[:, P * t:P * (t + 1)],
                                        rhs=picked_words[:, slots].bitcast(E2M1X4),
                                        rhs_scale=picked_plane[:, slots], start=True, stop=True)
                nc.scalar.copy(rounded[:, PACK * HALF * h:PACK * HALF * (h + 1)].rearrange("q (j t) -> q j t", t=PACK),
                               bank[:].rearrange("q t j -> q j t"))
            return rounded

        a_bf = first_stage("a", l1, w_raw, ws_rows, ws, E4M3X4, None, "ka_rows")
        b_bf = first_stage("b", l2, w2_raw, w2s_rows, w2s, E5M2X4, "ws", "w_raw")

        ka_words, ka_plane = quantize("kaq", ka_bf[:], U, "xs")

        kb_bytes = sb_tile("gb", [P, PACK * U], U8, "w2s")
        kb_slices = sb_tile("kb_rows", [P, PACK * U], BF16, "b_gw")
        entries = [slice(HALF // GROUP * c, HALF // GROUP * (c + 1)) for c in range(2)]
        for c in range(2):
            for t in range(PACK):
                at = slice(HALF * (PACK * c + t), HALF * (PACK * c + t + 1))
                nc.vector.tensor_copy(kb_bytes[:, at], cb_t[t][:].indirect(l4[:, entries[c]]))
                nc.scalar.activation(kb_slices[:, at], kb_bytes[:, at].bitcast(F8), COPY, scale=sb_t[:, t:t + 1])

        def quantize_kb(c):
            kb_bf = sb_tile(f"kb{c}_il", [P, PACK * HALF], BF16, "kb0_il")
            half = kb_slices[:, PACK * HALF * c:PACK * HALF * (c + 1)]
            nc.vector.tensor_copy(kb_bf[:].rearrange("q (c i t) -> q c t i", i=RUN, t=PACK),
                                  half.rearrange("q (t c i) -> q c t i", t=PACK, i=RUN))
            return quantize(f"kbq{c}", kb_bf[:], HALF)

        def score_and_put(c, kb_words, kb_plane, copy_out):
            candidates = slice(HALF * c, HALF * (c + 1))
            for h in range(2):
                slots = slice(HALF * h, HALF * (h + 1))
                bank = psum.tile([P, HALF], F32, name=f"p_bank{c}{h}")
                nc.tensor.matmul_mx(out=bank[:], lhsT=b_words[:, slots].bitcast(E4M3X4), lhsT_scale=b_plane[:, slots],
                                    rhs=kb_words[:].bitcast(E4M3X4), rhs_scale=kb_plane[:], start=True, stop=False)
                nc.tensor.matmul_mx(out=bank[:], lhsT=a_words[:, slots].bitcast(E4M3X4), lhsT_scale=a_plane[:, slots],
                                    rhs=ka_words[:, candidates].bitcast(E4M3X4), rhs_scale=ka_plane[:, candidates],
                                    start=False, stop=True)
                scores = sb_tile(f"p{c}{h}", [P, HALF], F32)
                copy_out(scores[:], bank[:])
                nc.scalar.activation(pages[h][:].indirect(l5[:, entries[c]]), scores[:], COPY, scale=sz_t[:, h:h + 1])

        a_words, a_plane = quantize("aq", a_bf[:], J)
        first_kb = quantize_kb(0)
        b_words, b_plane = quantize("bq", b_bf[:], J)

        score_and_put(0, *first_kb, nc.scalar.copy)
        score_and_put(1, *quantize_kb(1), nc.vector.tensor_copy)
        for h in range(2):
            nc.sync.dma_start(out[HALF * h:HALF * (h + 1), :], pages[h][:])
